import numpy as np, ml_dtypes
CORES = [1,17,65,89,97,113]
N = 6
import mx_ref
NC, NZ = 256, 128
BF = ml_dtypes.bfloat16
def setup_inputs(rng):
    def f(*shape):
        return mx_ref.flush((rng.standard_normal(shape, dtype=np.float32) * np.exp2(rng.integers(-2, 3, shape[:-1] + (1,)))).astype(BF))
    return {"w": f(N, 128, 512), "x": f(N, 128, 4 * NC), "d": f(N, 128, N * 512), "z": f(N, 128, 4 * NZ)}
def setup_inputs_blocks(rng):
    d = setup_inputs(rng)
    for k in ("w", "x", "d", "z"): d[k] = mx_ref.spread(d[k], rng, 2)
    return d
def setup_inputs_wide(rng):
    d = setup_inputs(rng)
    for k in ("w", "x", "d", "z"): d[k] = mx_ref.flush((d[k].astype(np.float32) * np.exp2(rng.integers(-8, 9, (N, 1, 1))).astype(np.float32)).astype(BF))
    return d
def setup_inputs_zeros(rng):
    d = setup_inputs(rng); v = d["x"].reshape(N, 128, -1, 4).copy()
    v[np.broadcast_to((rng.random((N, 1, v.shape[2], 1)) < 0.33), v.shape)] = 0
    d["x"] = v.reshape(d["x"].shape)
    return d
def reference(w, x, d, z):
    QX = [mx_ref.quantize(x[j]) for j in range(N)]; QZ = [mx_ref.quantize(z[j]) for j in range(N)]
    y = np.zeros((N, 128, N * NC), np.float32); h = np.zeros((N, 128, NZ), np.float32)
    for r in range(N):
        qw = mx_ref.quantize(w[r])
        for j in range(N):
            y[r][:, NC * j:NC * j + NC] = mx_ref.matmul(qw, QX[j])
            p = mx_ref.matmul(mx_ref.quantize(d[r][:, 512 * j:512 * j + 512]), QZ[j])
            h[r] = p if j == 0 else h[r] + p
    return {"y": y, "h": h}

@@ -1,0 +1,173 @@
+from concourse.bass import DstId, RemoteDMATransfer
+from concourse.mybir import dt, ActivationFunctionType
+
+N = 6
+XW, ZW = 256, 128
+SLOT = XW + ZW
+DW = 128
+
+SCRATCH = {
+    "xb": ("sbuf", [128, 4 * XW], "bfloat16"),
+    "zb": ("sbuf", [128, 4 * ZW], "bfloat16"),
+    "wb": ("sbuf", [128, 4 * DW], "bfloat16"),
+    "db": ("sbuf", [128, 4 * DW * N], "bfloat16"),
+    "qc": ("sbuf", [128, N * SLOT], "float8_e4m3fn_x4"),
+    "qs": ("sbuf", [128, N * SLOT], "uint8"),
+    "wq": ("sbuf", [128, DW], "float8_e4m3fn_x4"),
+    "ws": ("sbuf", [128, DW], "uint8"),
+    "dq": ("sbuf", [128, N * DW], "float8_e4m3fn_x4"),
+    "ds": ("sbuf", [128, N * DW], "uint8"),
+    "yo": ("sbuf", [128, N * XW], "float32"),
+    "ho": ("sbuf", [128, ZW], "float32"),
+    "py": ("psum", [128, 512 * N], "float32"),
+    "ph": ("psum", [128, 512], "float32"),
+}
+SEMAPHORES = (["ldz", "ldx", "ldw", "ldd0", "ldd1", "qz", "qx", "qw", "qd0", "qd1",
+               "fed", "fout", "sent", "hm", "hev", "sta", "stb"]
+              + ["arr%d" % j for j in range(N)] + ["mm%d" % k for k in range(N)] + ["ev%d" % k for k in range(N)])
+
+
+def _engines(mask):
+    return [e for e in range(mask.bit_length()) if (mask >> e) & 1]
+
+
+def _mask_of(engines):
+    return sum(1 << e for e in engines)
+
+
+def _helpers(cores, j, topo):
+    src = cores[j]
+    others = [c for c in cores if c != src]
+    cand = [c for c in range(topo.CHIPS * topo.CORES_PER_CHIP)
+            if topo.chip(c) == topo.chip(src) and c not in cores and all(topo.may_write(c, d) for d in others)]
+    near = [c for c in cand if topo.die(c) == topo.die(src)]
+    far = [c for c in cand if topo.die(c) != topo.die(src)]
+    return [near[0], far[0], far[1], near[1]]
+
+
+def _piece(T, j, p):
+    s = j * SLOT
+    if p < 3:
+        return T.qc[:, s + 128 * p:s + 128 * p + 128].bitcast(dt.uint8)
+    return T.qs[:, s:s + SLOT]
+
+
+def _forward(g, core, T, topo, cores, j, p):
+    feed = len(_engines(topo.mask(cores[j], core))) // 4
+    g.wait_ge(T.sem.fed, feed)
+    total = 0
+    for k in range(1, N):
+        dst = cores[(j + k) % N]
+        rid, pid, _ = topo.addr(dst)
+        m = topo.mask(core, dst)
+        g.remote_dma(out_ap=_piece(T, j, p), in_ap=_piece(T, j, p), remote_sem=T.sem["arr%d" % j],
+                     local_sem=T.sem.sent, pid=pid, routing_id=rid, dma_engine_mask=m)
+        total += len(_engines(m))
+    g.wait_ge(T.sem.sent, total)
+
+
+def rank_program(g, core, T, topo):
+    cores = list(T.cores)
+    r = T.rank_of(core)
+    if r is None:
+        for j in range(N):
+            hs = _helpers(cores, j, topo)
+            if core in hs:
+                _forward(g, core, T, topo, cores, j, hs.index(core))
+        return
+
+    S = T.sem
+    s = r * SLOT
+    half = N // 2 * DW
+
+    g.sync.dma_start(T.zb[:], T.z[:]).then_inc(S.ldz, 16)
+    g.scalar.dma_start(T.xb[:], T.x[:]).then_inc(S.ldx, 16)
+    g.sync.dma_start(T.wb[:], T.w[:]).then_inc(S.ldw, 16)
+
+    v = g.vector
+    v.wait_ge(S.ldz, 16)
+    v.quantize_mx(T.qc[:, s + XW:s + SLOT], T.qs[:, s + XW:s + SLOT], T.zb[:]).then_inc(S.qz, 1)
+    v.wait_ge(S.ldx, 16)
+    v.quantize_mx(T.qc[:, s:s + XW], T.qs[:, s:s + XW], T.xb[:]).then_inc(S.qx, 1)
+    v.wait_ge(S.ldw, 16)
+    v.quantize_mx(T.wq[:], T.ws[:], T.wb[:]).then_inc(S.qw, 1)
+
+    hs = _helpers(cores, r, topo)
+    g.wait_ge(S.qz, 1)
+    g.wait_ge(S.qx, 1)
+    trs, left = [], 0
+    for p, h in enumerate(hs):
+        es = _engines(topo.mask(core, h))
+        q = len(es) // 4
+        rid, pid, _ = topo.addr(h)
+        trs.append(RemoteDMATransfer(dst_ids=[DstId(rid=rid, pnc=pid)], dma_engine_mask=_mask_of(es[q * p:q * p + q]),
+                                     remote_sem=S.fed, src=_piece(T, r, p), dst=_piece(T, r, p)))
+        left += q
+    g.remote_dma_fused(trs[:3], local_sem=S.fout)
+    g.remote_dma_fused(trs[3:], local_sem=S.fout)
+
+    g.sync.wait_ge(S.fout, left)
+    g.sync.dma_start(T.db[:, 0:4 * half], T.d[:, 0:4 * half]).then_inc(S.ldd0, 16)
+    g.scalar.wait_ge(S.fout, left)
+    g.scalar.dma_start(T.db[:, 4 * half:8 * half], T.d[:, 4 * half:8 * half]).then_inc(S.ldd1, 16)
+    g.wait_ge(S.fout, left)
+    v.wait_ge(S.ldd0, 16)
+    v.quantize_mx(T.dq[:, 0:half], T.ds[:, 0:half], T.db[:, 0:4 * half]).then_inc(S.qd0, 1)
+    v.wait_ge(S.ldd1, 16)
+    v.quantize_mx(T.dq[:, half:2 * half], T.ds[:, half:2 * half], T.db[:, 4 * half:8 * half]).then_inc(S.qd1, 1)
+
+    te = g.tensor
+    order = [(r - k) % N for k in range(N)]
+    arrive = sum(len(_engines(topo.mask(h, core))) for h in _helpers(cores, order[1], topo))
+
+    def y_mm(k):
+        j = order[k]
+        te.matmul_mx(T.py[:, 512 * k:512 * k + XW], T.wq[:], T.ws[:],
+                     T.qc[:, j * SLOT:j * SLOT + XW], T.qs[:, j * SLOT:j * SLOT + XW], True, True).then_inc(S["mm%d" % k], 1)
+
+    def h_mm(k):
+        j = order[k]
+        i = te.matmul_mx(T.ph[:, 0:ZW], T.dq[:, j * DW:j * DW + DW], T.ds[:, j * DW:j * DW + DW],
+                         T.qc[:, j * SLOT + XW:j * SLOT + SLOT], T.qs[:, j * SLOT + XW:j * SLOT + SLOT],
+                         k == 0, k == N - 1)
+        if k == N - 1:
+            i.then_inc(S.hm, 1)
+
+    te.wait_ge(S.qw, 1)
+    te.wait_ge(S.qx, 1)
+    y_mm(0)
+    te.wait_ge(S["arr%d" % order[1]], arrive)
+    y_mm(1)
+    te.wait_ge(S.qz, 1)
+    te.wait_ge(S.qd0, 1)
+    te.wait_ge(S.qd1, 1)
+    h_mm(0)
+    h_mm(1)
+    for k in range(2, N):
+        te.wait_ge(S["arr%d" % order[k]], arrive)
+        y_mm(k)
+        h_mm(k)
+
+    na = nb = 0
+    for k in range(N):
+        j = order[k]
+        bank, out = T.py[:, 512 * k:512 * k + XW], T.yo[:, j * XW:j * XW + XW]
+        if k % 2:
+            v.wait_ge(S["mm%d" % k], 1)
+            v.tensor_copy(out, bank).then_inc(S["ev%d" % k], 1)
+            g.sync.wait_ge(S["ev%d" % k], 1)
+            g.sync.dma_start(T.y[:, j * XW:j * XW + XW], out).then_inc(S.sta, 16)
+            na += 16
+        else:
+            g.scalar.wait_ge(S["mm%d" % k], 1)
+            g.scalar.activation(out, bank, ActivationFunctionType.Copy).then_inc(S["ev%d" % k], 1)
+            g.scalar.wait_ge(S["ev%d" % k], 1)
+            g.scalar.dma_start(T.y[:, j * XW:j * XW + XW], out).then_inc(S.stb, 16)
+            nb += 16
+    g.scalar.wait_ge(S.hm, 1)
+    g.scalar.activation(T.ho[:], T.ph[:, 0:ZW], ActivationFunctionType.Copy).then_inc(S.hev, 1)
+    g.scalar.wait_ge(S.hev, 1)
+    g.scalar.dma_start(T.h[:], T.ho[:]).then_inc(S.stb, 16)
+    nb += 16
+    g.sync.wait_ge(S.sta, na)
+    g.scalar.wait_ge(S.stb, nb)

@@ -3,8 +3,11 @@ from concourse.mybir import dt, ActivationFunctionType
 
 N = 6
 XW, ZW = 256, 128
+XH = XW // 2
 SLOT = XW + ZW
 DW = 128
+NP = 5
+CARRIER = [0, 1, 2, 3, 2]
 
 SCRATCH = {
     "xb": ("sbuf", [128, 4 * XW], "bfloat16"),
@@ -22,9 +25,11 @@ SCRATCH = {
     "py": ("psum", [128, 512 * N], "float32"),
     "ph": ("psum", [128, 512], "float32"),
 }
-SEMAPHORES = (["ldz", "ldx", "ldw", "ldd0", "ldd1", "qz", "qx", "qw", "qd0", "qd1",
-               "fed", "fout", "sent", "hm", "hev", "sta", "stb"]
-              + ["arr%d" % j for j in range(N)] + ["mm%d" % k for k in range(N)] + ["ev%d" % k for k in range(N)])
+SEMAPHORES = (["ldz", "ldxl", "ldxh", "ldw", "ldd0", "ldd1", "qz", "qxl", "qxh", "qw", "qd0", "qd1",
+               "fout", "sent", "hm", "hev", "sta", "stb"]
+              + ["fed%d" % p for p in range(NP)]
+              + ["ax%d" % j for j in range(N)] + ["az%d" % j for j in range(N)]
+              + ["mm%d" % k for k in range(N)] + ["ev%d" % k for k in range(N)])
 
 
 def _engines(mask):
@@ -42,27 +47,42 @@ def _helpers(cores, j, topo):
             if topo.chip(c) == topo.chip(src) and c not in cores and all(topo.may_write(c, d) for d in others)]
     near = [c for c in cand if topo.die(c) == topo.die(src)]
     far = [c for c in cand if topo.die(c) != topo.die(src)]
-    return [near[0], far[0], far[1], near[1]]
+    return [far[0], near[0], near[1], far[1]]
 
 
 def _piece(T, j, p):
     s = j * SLOT
-    if p < 3:
-        return T.qc[:, s + 128 * p:s + 128 * p + 128].bitcast(dt.uint8)
-    return T.qs[:, s:s + SLOT]
+    if p == 0:
+        return T.qc[:, s:s + XH].bitcast(dt.uint8)
+    if p == 1:
+        return T.qc[:, s + XH:s + XW].bitcast(dt.uint8)
+    if p == 2:
+        return T.qs[:, s:s + XW]
+    if p == 3:
+        return T.qc[:, s + XW:s + SLOT].bitcast(dt.uint8)
+    return T.qs[:, s + XW:s + SLOT]
 
 
-def _forward(g, core, T, topo, cores, j, p):
-    feed = len(_engines(topo.mask(cores[j], core))) // 4
-    g.wait_ge(T.sem.fed, feed)
+def _feed_mask(topo, src, dst, p):
+    es = _engines(topo.mask(src, dst))
+    n = len(es) // 2
+    return _mask_of(es[n * (p % 2):n * (p % 2) + n])
+
+
+def _forward(g, core, T, topo, cores, j, idx):
     total = 0
-    for k in range(1, N):
-        dst = cores[(j + k) % N]
-        rid, pid, _ = topo.addr(dst)
-        m = topo.mask(core, dst)
-        g.remote_dma(out_ap=_piece(T, j, p), in_ap=_piece(T, j, p), remote_sem=T.sem["arr%d" % j],
-                     local_sem=T.sem.sent, pid=pid, routing_id=rid, dma_engine_mask=m)
-        total += len(_engines(m))
+    for p in range(NP):
+        if CARRIER[p] != idx:
+            continue
+        g.wait_ge(T.sem["fed%d" % p], len(_engines(_feed_mask(topo, cores[j], core, p))))
+        for k in range(1, N):
+            dst = cores[(j + k) % N]
+            rid, pid, _ = topo.addr(dst)
+            m = topo.mask(core, dst)
+            g.remote_dma(out_ap=_piece(T, j, p), in_ap=_piece(T, j, p),
+                         remote_sem=T.sem[("ax%d" if p < 3 else "az%d") % j],
+                         local_sem=T.sem.sent, pid=pid, routing_id=rid, dma_engine_mask=m)
+            total += len(_engines(m))
     g.wait_ge(T.sem.sent, total)
 
 
@@ -80,31 +100,33 @@ def rank_program(g, core, T, topo):
     s = r * SLOT
     half = N // 2 * DW
 
+    g.sync.dma_start(T.xb[:, 0:4 * XH], T.x[:, 0:4 * XH]).then_inc(S.ldxl, 16)
+    g.scalar.dma_start(T.xb[:, 4 * XH:4 * XW], T.x[:, 4 * XH:4 * XW]).then_inc(S.ldxh, 16)
     g.sync.dma_start(T.zb[:], T.z[:]).then_inc(S.ldz, 16)
-    g.scalar.dma_start(T.xb[:], T.x[:]).then_inc(S.ldx, 16)
-    g.sync.dma_start(T.wb[:], T.w[:]).then_inc(S.ldw, 16)
+    g.scalar.dma_start(T.wb[:], T.w[:]).then_inc(S.ldw, 16)
 
     v = g.vector
+    v.wait_ge(S.ldxl, 16)
+    v.quantize_mx(T.qc[:, s:s + XH], T.qs[:, s:s + XH], T.xb[:, 0:4 * XH]).then_inc(S.qxl, 1)
+    v.wait_ge(S.ldxh, 16)
+    v.quantize_mx(T.qc[:, s + XH:s + XW], T.qs[:, s + XH:s + XW], T.xb[:, 4 * XH:4 * XW]).then_inc(S.qxh, 1)
     v.wait_ge(S.ldz, 16)
     v.quantize_mx(T.qc[:, s + XW:s + SLOT], T.qs[:, s + XW:s + SLOT], T.zb[:]).then_inc(S.qz, 1)
-    v.wait_ge(S.ldx, 16)
-    v.quantize_mx(T.qc[:, s:s + XW], T.qs[:, s:s + XW], T.xb[:]).then_inc(S.qx, 1)
     v.wait_ge(S.ldw, 16)
     v.quantize_mx(T.wq[:], T.ws[:], T.wb[:]).then_inc(S.qw, 1)
 
     hs = _helpers(cores, r, topo)
-    g.wait_ge(S.qz, 1)
-    g.wait_ge(S.qx, 1)
-    trs, left = [], 0
-    for p, h in enumerate(hs):
-        es = _engines(topo.mask(core, h))
-        q = len(es) // 4
+    left = 0
+    ready = {0: S.qxl, 1: S.qxh, 3: S.qz}
+    for p in range(NP):
+        if p in ready:
+            g.wait_ge(ready[p], 1)
+        h = hs[CARRIER[p]]
         rid, pid, _ = topo.addr(h)
-        trs.append(RemoteDMATransfer(dst_ids=[DstId(rid=rid, pnc=pid)], dma_engine_mask=_mask_of(es[q * p:q * p + q]),
-                                     remote_sem=S.fed, src=_piece(T, r, p), dst=_piece(T, r, p)))
-        left += q
-    g.remote_dma_fused(trs[:3], local_sem=S.fout)
-    g.remote_dma_fused(trs[3:], local_sem=S.fout)
+        m = _feed_mask(topo, core, h, p)
+        g.remote_dma(out_ap=_piece(T, r, p), in_ap=_piece(T, r, p), remote_sem=S["fed%d" % p],
+                     local_sem=S.fout, pid=pid, routing_id=rid, dma_engine_mask=m)
+        left += len(_engines(m))
 
     g.sync.wait_ge(S.fout, left)
     g.sync.dma_start(T.db[:, 0:4 * half], T.d[:, 0:4 * half]).then_inc(S.ldd0, 16)
@@ -118,15 +140,21 @@ def rank_program(g, core, T, topo):
 
     te = g.tensor
     order = [(r - k) % N for k in range(N)]
-    arrive = sum(len(_engines(topo.mask(h, core))) for h in _helpers(cores, order[1], topo))
+    src_hs = _helpers(cores, order[1], topo)
+    per = [len(_engines(topo.mask(src_hs[CARRIER[p]], core))) for p in range(NP)]
+    nx, nz = sum(per[:3]), sum(per[3:])
 
     def y_mm(k):
         j = order[k]
+        if k:
+            te.wait_ge(S["ax%d" % j], nx)
         te.matmul_mx(T.py[:, 512 * k:512 * k + XW], T.wq[:], T.ws[:],
                      T.qc[:, j * SLOT:j * SLOT + XW], T.qs[:, j * SLOT:j * SLOT + XW], True, True).then_inc(S["mm%d" % k], 1)
 
     def h_mm(k):
         j = order[k]
+        if k:
+            te.wait_ge(S["az%d" % j], nz)
         i = te.matmul_mx(T.ph[:, 0:ZW], T.dq[:, j * DW:j * DW + DW], T.ds[:, j * DW:j * DW + DW],
                          T.qc[:, j * SLOT + XW:j * SLOT + SLOT], T.qs[:, j * SLOT + XW:j * SLOT + SLOT],
                          k == 0, k == N - 1)
@@ -134,19 +162,20 @@ def rank_program(g, core, T, topo):
             i.then_inc(S.hm, 1)
 
     te.wait_ge(S.qw, 1)
-    te.wait_ge(S.qx, 1)
-    y_mm(0)
-    te.wait_ge(S["arr%d" % order[1]], arrive)
-    y_mm(1)
+    te.wait_ge(S.qxl, 1)
+    te.wait_ge(S.qxh, 1)
+    for k in range(4):
+        y_mm(k)
     te.wait_ge(S.qz, 1)
     te.wait_ge(S.qd0, 1)
     te.wait_ge(S.qd1, 1)
-    h_mm(0)
-    h_mm(1)
-    for k in range(2, N):
-        te.wait_ge(S["arr%d" % order[k]], arrive)
-        y_mm(k)
+    for k in range(3):
         h_mm(k)
+    y_mm(4)
+    h_mm(3)
+    y_mm(5)
+    h_mm(4)
+    h_mm(5)
 
     na = nb = 0
     for k in range(N):

from concourse.bass import DstId, RemoteDMATransfer
from concourse.mybir import dt, ActivationFunctionType

N = 6
XW, ZW = 256, 128
XH = XW // 2
SLOT = XW + ZW
DW = 128
NP = 5
CARRIER = [0, 1, 2, 3, 2]

SCRATCH = {
    "xb": ("sbuf", [128, 4 * XW], "bfloat16"),
    "zb": ("sbuf", [128, 4 * ZW], "bfloat16"),
    "wb": ("sbuf", [128, 4 * DW], "bfloat16"),
    "db": ("sbuf", [128, 4 * DW * N], "bfloat16"),
    "qc": ("sbuf", [128, N * SLOT], "float8_e4m3fn_x4"),
    "qs": ("sbuf", [128, N * SLOT], "uint8"),
    "wq": ("sbuf", [128, DW], "float8_e4m3fn_x4"),
    "ws": ("sbuf", [128, DW], "uint8"),
    "dq": ("sbuf", [128, N * DW], "float8_e4m3fn_x4"),
    "ds": ("sbuf", [128, N * DW], "uint8"),
    "yo": ("sbuf", [128, N * XW], "float32"),
    "ho": ("sbuf", [128, ZW], "float32"),
    "py": ("psum", [128, 512 * N], "float32"),
    "ph": ("psum", [128, 512], "float32"),
}
SEMAPHORES = (["ldz", "ldxl", "ldxh", "ldw", "ldd0", "ldd1", "qz", "qxl", "qxh", "qw", "qd0", "qd1",
               "fout", "sent", "hm", "hev", "sta", "stb"]
              + ["fed%d" % p for p in range(NP)]
              + ["ax%d" % j for j in range(N)] + ["az%d" % j for j in range(N)]
              + ["mm%d" % k for k in range(N)] + ["ev%d" % k for k in range(N)])


def _engines(mask):
    return [e for e in range(mask.bit_length()) if (mask >> e) & 1]


def _mask_of(engines):
    return sum(1 << e for e in engines)


def _helpers(cores, j, topo):
    src = cores[j]
    others = [c for c in cores if c != src]
    cand = [c for c in range(topo.CHIPS * topo.CORES_PER_CHIP)
            if topo.chip(c) == topo.chip(src) and c not in cores and all(topo.may_write(c, d) for d in others)]
    near = [c for c in cand if topo.die(c) == topo.die(src)]
    far = [c for c in cand if topo.die(c) != topo.die(src)]
    return [far[0], near[0], near[1], far[1]]


def _piece(T, j, p):
    s = j * SLOT
    if p == 0:
        return T.qc[:, s:s + XH].bitcast(dt.uint8)
    if p == 1:
        return T.qc[:, s + XH:s + XW].bitcast(dt.uint8)
    if p == 2:
        return T.qs[:, s:s + XW]
    if p == 3:
        return T.qc[:, s + XW:s + SLOT].bitcast(dt.uint8)
    return T.qs[:, s + XW:s + SLOT]


def _feed_mask(topo, src, dst, p):
    es = _engines(topo.mask(src, dst))
    n = len(es) // 2
    return _mask_of(es[n * (p % 2):n * (p % 2) + n])


def _forward(g, core, T, topo, cores, j, idx):
    total = 0
    for p in range(NP):
        if CARRIER[p] != idx:
            continue
        g.wait_ge(T.sem["fed%d" % p], len(_engines(_feed_mask(topo, cores[j], core, p))))
        for k in range(1, N):
            dst = cores[(j + k) % N]
            rid, pid, _ = topo.addr(dst)
            m = topo.mask(core, dst)
            g.remote_dma(out_ap=_piece(T, j, p), in_ap=_piece(T, j, p),
                         remote_sem=T.sem[("ax%d" if p < 3 else "az%d") % j],
                         local_sem=T.sem.sent, pid=pid, routing_id=rid, dma_engine_mask=m)
            total += len(_engines(m))
    g.wait_ge(T.sem.sent, total)


def rank_program(g, core, T, topo):
    cores = list(T.cores)
    r = T.rank_of(core)
    if r is None:
        for j in range(N):
            hs = _helpers(cores, j, topo)
            if core in hs:
                _forward(g, core, T, topo, cores, j, hs.index(core))
        return

    S = T.sem
    s = r * SLOT
    half = N // 2 * DW

    g.sync.dma_start(T.xb[:, 0:4 * XH], T.x[:, 0:4 * XH]).then_inc(S.ldxl, 16)
    g.scalar.dma_start(T.xb[:, 4 * XH:4 * XW], T.x[:, 4 * XH:4 * XW]).then_inc(S.ldxh, 16)
    g.sync.dma_start(T.zb[:], T.z[:]).then_inc(S.ldz, 16)
    g.scalar.dma_start(T.wb[:], T.w[:]).then_inc(S.ldw, 16)

    v = g.vector
    v.wait_ge(S.ldxl, 16)
    v.quantize_mx(T.qc[:, s:s + XH], T.qs[:, s:s + XH], T.xb[:, 0:4 * XH]).then_inc(S.qxl, 1)
    v.wait_ge(S.ldxh, 16)
    v.quantize_mx(T.qc[:, s + XH:s + XW], T.qs[:, s + XH:s + XW], T.xb[:, 4 * XH:4 * XW]).then_inc(S.qxh, 1)
    v.wait_ge(S.ldz, 16)
    v.quantize_mx(T.qc[:, s + XW:s + SLOT], T.qs[:, s + XW:s + SLOT], T.zb[:]).then_inc(S.qz, 1)
    v.wait_ge(S.ldw, 16)
    v.quantize_mx(T.wq[:], T.ws[:], T.wb[:]).then_inc(S.qw, 1)

    hs = _helpers(cores, r, topo)
    left = 0
    ready = {0: S.qxl, 1: S.qxh, 3: S.qz}
    for p in range(NP):
        if p in ready:
            g.wait_ge(ready[p], 1)
        h = hs[CARRIER[p]]
        rid, pid, _ = topo.addr(h)
        m = _feed_mask(topo, core, h, p)
        g.remote_dma(out_ap=_piece(T, r, p), in_ap=_piece(T, r, p), remote_sem=S["fed%d" % p],
                     local_sem=S.fout, pid=pid, routing_id=rid, dma_engine_mask=m)
        left += len(_engines(m))

    g.sync.wait_ge(S.fout, left)
    g.sync.dma_start(T.db[:, 0:4 * half], T.d[:, 0:4 * half]).then_inc(S.ldd0, 16)
    g.scalar.wait_ge(S.fout, left)
    g.scalar.dma_start(T.db[:, 4 * half:8 * half], T.d[:, 4 * half:8 * half]).then_inc(S.ldd1, 16)
    g.wait_ge(S.fout, left)
    v.wait_ge(S.ldd0, 16)
    v.quantize_mx(T.dq[:, 0:half], T.ds[:, 0:half], T.db[:, 0:4 * half]).then_inc(S.qd0, 1)
    v.wait_ge(S.ldd1, 16)
    v.quantize_mx(T.dq[:, half:2 * half], T.ds[:, half:2 * half], T.db[:, 4 * half:8 * half]).then_inc(S.qd1, 1)

    te = g.tensor
    order = [(r - k) % N for k in range(N)]
    src_hs = _helpers(cores, order[1], topo)
    per = [len(_engines(topo.mask(src_hs[CARRIER[p]], core))) for p in range(NP)]
    nx, nz = sum(per[:3]), sum(per[3:])

    def y_mm(k):
        j = order[k]
        if k:
            te.wait_ge(S["ax%d" % j], nx)
        te.matmul_mx(T.py[:, 512 * k:512 * k + XW], T.wq[:], T.ws[:],
                     T.qc[:, j * SLOT:j * SLOT + XW], T.qs[:, j * SLOT:j * SLOT + XW], True, True).then_inc(S["mm%d" % k], 1)

    def h_mm(k):
        j = order[k]
        if k:
            te.wait_ge(S["az%d" % j], nz)
        i = te.matmul_mx(T.ph[:, 0:ZW], T.dq[:, j * DW:j * DW + DW], T.ds[:, j * DW:j * DW + DW],
                         T.qc[:, j * SLOT + XW:j * SLOT + SLOT], T.qs[:, j * SLOT + XW:j * SLOT + SLOT],
                         k == 0, k == N - 1)
        if k == N - 1:
            i.then_inc(S.hm, 1)

    te.wait_ge(S.qw, 1)
    te.wait_ge(S.qxl, 1)
    te.wait_ge(S.qxh, 1)
    for k in range(4):
        y_mm(k)
    te.wait_ge(S.qz, 1)
    te.wait_ge(S.qd0, 1)
    te.wait_ge(S.qd1, 1)
    for k in range(3):
        h_mm(k)
    y_mm(4)
    h_mm(3)
    y_mm(5)
    h_mm(4)
    h_mm(5)

    na = nb = 0
    for k in range(N):
        j = order[k]
        bank, out = T.py[:, 512 * k:512 * k + XW], T.yo[:, j * XW:j * XW + XW]
        if k % 2:
            v.wait_ge(S["mm%d" % k], 1)
            v.tensor_copy(out, bank).then_inc(S["ev%d" % k], 1)
            g.sync.wait_ge(S["ev%d" % k], 1)
            g.sync.dma_start(T.y[:, j * XW:j * XW + XW], out).then_inc(S.sta, 16)
            na += 16
        else:
            g.scalar.wait_ge(S["mm%d" % k], 1)
            g.scalar.activation(out, bank, ActivationFunctionType.Copy).then_inc(S["ev%d" % k], 1)
            g.scalar.wait_ge(S["ev%d" % k], 1)
            g.scalar.dma_start(T.y[:, j * XW:j * XW + XW], out).then_inc(S.stb, 16)
            nb += 16
    g.scalar.wait_ge(S.hm, 1)
    g.scalar.activation(T.ho[:], T.ph[:, 0:ZW], ActivationFunctionType.Copy).then_inc(S.hev, 1)
    g.scalar.wait_ge(S.hev, 1)
    g.scalar.dma_start(T.h[:], T.ho[:]).then_inc(S.stb, 16)
    nb += 16
    g.sync.wait_ge(S.sta, na)
    g.scalar.wait_ge(S.stb, nb)
